import numpy as np
import ml_dtypes


def mxq(x, axis, fmt="e4m3"):
    dtype, down = {"e4m3": (ml_dtypes.float8_e4m3fn, 7), "e5m2": (ml_dtypes.float8_e5m2, 14)}[fmt]
    v = np.moveaxis(np.asarray(x, np.float32).astype(ml_dtypes.bfloat16).astype(np.float64), axis, -1)
    blocks = v.reshape(v.shape[:-1] + (-1, 32))
    amax = np.abs(blocks).max(-1, keepdims=True)
    byte = np.maximum(np.where(amax > 0, np.frexp(amax)[1] - 1 + 127, 0) - down, 1)
    scale = np.exp2(byte - 127.0)
    codes = (blocks / scale).astype(np.float32).astype(dtype).astype(np.float64)
    return np.moveaxis((codes * scale).reshape(v.shape), -1, axis)


WIDE = False


def mx_kscale(k):
    if not WIDE:
        return np.ones(k)
    levels = np.array([10, -10, 5, -5, 0])
    if k % 512:
        return np.exp2(np.random.permutation(np.resize(levels, k // 32))).repeat(32)
    a = np.empty((k // 512, 16))
    for p in range(k // 512):
        a[p, :8] = np.random.permutation(np.resize(levels, 8))
        for g in range(8):
            far = levels[np.abs(levels - a[p, g]) >= 10]
            a[p, g + 8] = far[np.random.randint(len(far))]
    return np.exp2(a.ravel()).repeat(32)


def f64(x):
    return np.asarray(x).astype(np.float64)


def striped(idx):
    return np.tile(idx.reshape(-1, 16).T, (8, 1)).astype(np.uint16)


def unstriped(offs):
    return offs[:16].T.reshape(-1).astype(np.int64)


def pack_weight(w):
    k, n = w.shape
    w = f64(np.asarray(w, np.float32).astype(ml_dtypes.bfloat16)).reshape(k // 32, 32, n)
    amax = np.abs(w).max(1)
    byte = np.clip(np.where(amax > 0, np.frexp(amax)[1] - 1 + 127 - 7, 1), 1, 254)
    scaled = (w * np.exp2(127.0 - byte)[:, None, :]).reshape(k, n).astype(np.float32)
    words = np.ascontiguousarray(scaled.reshape(k // 512, 128, 4, n).transpose(0, 1, 3, 2)).astype(ml_dtypes.float8_e4m3fn).view(np.uint8)
    return words, np.ascontiguousarray(byte.astype(np.uint8).reshape(k // 512, 16, n))


def unpack_weight(words, scales):
    g, p, n, _ = words.shape
    vals = np.ascontiguousarray(words).view(ml_dtypes.float8_e4m3fn).astype(np.float64) * np.repeat(np.exp2(scales.astype(np.float64) - 127.0), 8, axis=1)[..., None]
    return vals.transpose(0, 1, 3, 2).reshape(g * 512, n)


def relu(v):
    return np.maximum(v, 0.0)


K, T, S, N, D = 1024, 2048, 1024, 256, 8


def setup_inputs():
    n = np.random.standard_normal
    s = mx_kscale(K)[:, None]
    packed_xT = pack_weight(n((K, T)) * s)
    return {
        "x_words": packed_xT[0],
        "x_scales": packed_xT[1],
        "w1": (n((K, N)) / np.sqrt(K) / s).astype(np.float32),
        "bias": (0.3 * n((N, 1))).astype(np.float32),
        "offs": striped(np.random.permutation(T)[:S]),
    }


def reference(x_words, x_scales, w1, bias, offs):
    xq = unpack_weight(x_words, x_scales)[:, unstriped(offs)]
    y = np.log(relu((mxq(f64(w1), 0, "e4m3").T @ xq) + f64(bias)) + 1.0)
    return y.reshape(len(y), -1, D).sum(axis=2)

@@ -1,0 +1,119 @@
+from contextlib import ExitStack
+
+import concourse.mybir as mybir
+
+K, T, S, N, D = 1024, 2048, 1024, 256, 8
+FLOPS = 2 * K * N * S
+
+F32 = mybir.dt.float32
+BF16 = mybir.dt.bfloat16
+I32 = mybir.dt.int32
+U32 = mybir.dt.uint32
+U16 = mybir.dt.uint16
+U8 = mybir.dt.uint8
+FP8X4 = mybir.dt.float8_e4m3fn_x4
+ACT = mybir.ActivationFunctionType
+ALU = mybir.AluOpType
+
+P = 128
+PACK = 4
+PASSES = K // (P * PACK)
+TERM_TILES = N // P
+CHUNK = 256
+CHUNKS = S // CHUNK
+HALF = S // 2
+LANES = 16
+VECTOR_RELU = 2
+
+
+def tile_picked_ysplade_sum_p_kernel(tc, x_words, x_scales, w1, bias, offs, out):
+    nc = tc.nc
+    with ExitStack() as ctx:
+        keep = ctx.enter_context(tc.tile_pool(name="keep", bufs=1))
+        psum = ctx.enter_context(tc.psum_pool(name="psum", bufs=1))
+
+        offsets = keep.tile([P, S // LANES], U16, name="offsets")
+        word_table = [keep.tile([P, T], U32, name=f"word_table{o}", align_bytes=64) for o in range(PASSES)]
+        scale_table = keep.tile([P, T], U8, name="scale_table", tag="shared", align_bytes=64)
+        w_raw = [keep.tile([P, PACK, N], F32, name=f"w_raw{o}", align_bytes=64) for o in range(PASSES)]
+        bias_cols = keep.tile([P, TERM_TILES], F32, name="bias_cols")
+        warm_in = keep.tile([P, 1], F32, name="warm_in")
+        warm_out = keep.tile([P, 1], F32, name="warm_out")
+
+        nc.vector.memset(scale_table[:].bitcast(I32), 0)
+        nc.vector.memset(warm_in[:], 1.0)
+        nc.scalar.activation(warm_out[:], warm_in[:], ACT.Ln, bias=1.0)
+
+        def load_words(o):
+            nc.sync.dma_start(out=word_table[o][:].bitcast(I32), in_=x_words[o].rearrange("p n t -> p (n t)").bitcast(I32))
+
+        load_words(0)
+        nc.sync.dma_start(offsets[:], offs)
+        for q in range(4):
+            nc.gpsimd.dma_start(out=scale_table[32 * q : 32 * q + 4 * PASSES, :].bitcast(I32), in_=x_scales[:, 4 * q : 4 * q + 4, :].bitcast(I32))
+        for o in range(PASSES):
+            nc.sync.dma_start(out=w_raw[o][:], in_=w1[512 * o : 512 * (o + 1), :].rearrange("(p j) m -> p j m", j=PACK))
+        load_words(1)
+        with nc.allow_non_contiguous_dma(reason="one bias value a partition"):
+            nc.scalar.dma_start(out=bias_cols[:], in_=bias.rearrange("(t p) o -> p (t o)", p=P))
+
+        w_codes = [keep.tile([P, N], U32, name=f"w_codes{o}", align_bytes=64) for o in range(PASSES)]
+        w_scales = [keep.tile([P, N], U8, name=f"w_scales{o}", align_bytes=64) for o in range(PASSES)]
+        w_grouped = [keep.tile([P, N, PACK], BF16, name=f"w_grouped{o}", align_bytes=64) for o in range(PASSES)]
+        for o in range(PASSES):
+            nc.scalar.copy(out=w_grouped[o][:], in_=w_raw[o][:].rearrange("p j m -> p m j"))
+
+        def quantize(o):
+            nc.vector.quantize_mx(out=w_codes[o][:].bitcast(FP8X4), scales=w_scales[o][:], in_=w_grouped[o][:].rearrange("p m j -> p (m j)"))
+
+        def picked(table, start, count):
+            return table[:].indirect(offsets[:, start // LANES : (start + count) // LANES])
+
+        words = [keep.tile([P, S], U32, name="words0", align_bytes=64)]
+        scales = [keep.tile([P, HALF], U8, name=f"scales{h}", align_bytes=64) for h in range(2)]
+        acc = [[psum.tile([P, CHUNK], F32, name=f"acc{c}_{t}") for t in range(TERM_TILES)] for c in range(CHUNKS)]
+
+        def multiply(o, c):
+            cols = slice((c * CHUNK) % HALF, (c * CHUNK) % HALF + CHUNK)
+            moving = words[o][:, c * CHUNK : (c + 1) * CHUNK]
+            for t in range(TERM_TILES):
+                nc.tensor.matmul_mx(
+                    out=acc[c][t][:],
+                    lhsT=w_codes[o][:, t * P : (t + 1) * P].bitcast(FP8X4),
+                    lhsT_scale=w_scales[o][:, t * P : (t + 1) * P],
+                    rhs=moving.bitcast(FP8X4),
+                    rhs_scale=scales[c * CHUNK // HALF][4 * o : P, cols],
+                    start=(o == 0),
+                    stop=(o == PASSES - 1),
+                )
+
+        nc.vector.tensor_copy(words[0][:], picked(word_table[0], 0, S))
+        quantize(0)
+        for h in range(2):
+            nc.vector.tensor_copy(scales[h][:], picked(scale_table, h * HALF, HALF))
+            for c in range(h * CHUNKS // 2, (h + 1) * CHUNKS // 2):
+                multiply(0, c)
+        quantize(1)
+        words.append(keep.tile([P, S], U32, name="words1", tag="shared", align_bytes=64))
+        for c in range(CHUNKS):
+            nc.vector.tensor_copy(words[1][:, c * CHUNK : (c + 1) * CHUNK], picked(word_table[1], c * CHUNK, CHUNK))
+            multiply(1, c)
+
+        result = keep.tile([P, TERM_TILES, S // D], F32, name="result")
+        docs = CHUNK // D
+        for c in range(CHUNKS):
+            active = keep.tile([P, TERM_TILES, CHUNK], F32, name=f"active{c}")
+            logged = keep.tile([P, TERM_TILES, CHUNK], F32, name=f"logged{c}")
+            for t in range(TERM_TILES):
+                if c * TERM_TILES + t >= CHUNKS * TERM_TILES - VECTOR_RELU:
+                    nc.vector.tensor_scalar(active[:, t, :], acc[c][t][:], bias_cols[:, t : t + 1], 0.0, ALU.add, ALU.max)
+                else:
+                    nc.scalar.activation(active[:, t, :], acc[c][t][:], ACT.Relu, bias=bias_cols[:, t : t + 1])
+            nc.scalar.activation(logged[:], active[:], ACT.Ln, bias=1.0)
+            nc.vector.tensor_reduce(
+                result[:, :, c * docs : (c + 1) * docs],
+                logged[:].rearrange("p t (v d) -> p t v d", d=D),
+                mybir.AxisListType.X,
+                ALU.add,
+            )
+        nc.sync.dma_start(out=out.rearrange("(t p) v -> p t v", p=P), in_=result[:])

@@ -23,7 +23,8 @@ CHUNK = 256
 CHUNKS = S // CHUNK
 HALF = S // 2
 LANES = 16
-VECTOR_RELU = 2
+VECTOR_RELU = 3
+GPSIMD_SUMS = 0
 
 
 def tile_picked_ysplade_sum_p_kernel(tc, x_words, x_scales, w1, bias, offs, out):
@@ -34,28 +35,30 @@ def tile_picked_ysplade_sum_p_kernel(tc, x_words, x_scales, w1, bias, offs, out)
 
         offsets = keep.tile([P, S // LANES], U16, name="offsets")
         word_table = [keep.tile([P, T], U32, name=f"word_table{o}", align_bytes=64) for o in range(PASSES)]
-        scale_table = keep.tile([P, T], U8, name="scale_table", tag="shared", align_bytes=64)
+        scale_table = keep.tile([P, T], U8, name="scale_table", align_bytes=64)
         w_raw = [keep.tile([P, PACK, N], F32, name=f"w_raw{o}", align_bytes=64) for o in range(PASSES)]
         bias_cols = keep.tile([P, TERM_TILES], F32, name="bias_cols")
         warm_in = keep.tile([P, 1], F32, name="warm_in")
         warm_out = keep.tile([P, 1], F32, name="warm_out")
 
-        nc.vector.memset(scale_table[:].bitcast(I32), 0)
-        nc.vector.memset(warm_in[:], 1.0)
-        nc.scalar.activation(warm_out[:], warm_in[:], ACT.Ln, bias=1.0)
-
         def load_words(o):
             nc.sync.dma_start(out=word_table[o][:].bitcast(I32), in_=x_words[o].rearrange("p n t -> p (n t)").bitcast(I32))
 
-        load_words(0)
-        nc.sync.dma_start(offsets[:], offs)
-        for q in range(4):
-            nc.gpsimd.dma_start(out=scale_table[32 * q : 32 * q + 4 * PASSES, :].bitcast(I32), in_=x_scales[:, 4 * q : 4 * q + 4, :].bitcast(I32))
-        for o in range(PASSES):
+        def load_weights(o):
             nc.sync.dma_start(out=w_raw[o][:], in_=w1[512 * o : 512 * (o + 1), :].rearrange("(p j) m -> p j m", j=PACK))
+
+        nc.vector.memset(scale_table[:].bitcast(I32), 0)
+        for q in range(4):
+            nc.scalar.dma_start(out=scale_table[32 * q : 32 * q + 4 * PASSES, :].bitcast(I32), in_=x_scales[:, 4 * q : 4 * q + 4, :].bitcast(I32))
+        nc.vector.memset(warm_in[:], 1.0)
+        nc.scalar.activation(warm_out[:], warm_in[:], ACT.Ln, bias=1.0)
+        load_weights(0)
+        nc.sync.dma_start(offsets[:], offs)
+        load_words(0)
+        load_weights(1)
         load_words(1)
         with nc.allow_non_contiguous_dma(reason="one bias value a partition"):
-            nc.scalar.dma_start(out=bias_cols[:], in_=bias.rearrange("(t p) o -> p (t o)", p=P))
+            nc.sync.dma_start(out=bias_cols[:], in_=bias.rearrange("(t p) o -> p (t o)", p=P))
 
         w_codes = [keep.tile([P, N], U32, name=f"w_codes{o}", align_bytes=64) for o in range(PASSES)]
         w_scales = [keep.tile([P, N], U8, name=f"w_scales{o}", align_bytes=64) for o in range(PASSES)]
@@ -69,51 +72,70 @@ def tile_picked_ysplade_sum_p_kernel(tc, x_words, x_scales, w1, bias, offs, out)
         def picked(table, start, count):
             return table[:].indirect(offsets[:, start // LANES : (start + count) // LANES])
 
-        words = [keep.tile([P, S], U32, name="words0", align_bytes=64)]
+        words0 = [keep.tile([P, HALF], U32, name=f"words0_{h}", align_bytes=64) for h in range(2)]
+        words1 = [keep.tile([P, CHUNK], U32, name=f"words1_{c}", align_bytes=64) for c in range(CHUNKS)]
         scales = [keep.tile([P, HALF], U8, name=f"scales{h}", align_bytes=64) for h in range(2)]
         acc = [[psum.tile([P, CHUNK], F32, name=f"acc{c}_{t}") for t in range(TERM_TILES)] for c in range(CHUNKS)]
 
         def multiply(o, c):
+            h = c * CHUNK // HALF
             cols = slice((c * CHUNK) % HALF, (c * CHUNK) % HALF + CHUNK)
-            moving = words[o][:, c * CHUNK : (c + 1) * CHUNK]
+            moving = words0[h][:, cols] if o == 0 else words1[c][:]
             for t in range(TERM_TILES):
                 nc.tensor.matmul_mx(
                     out=acc[c][t][:],
                     lhsT=w_codes[o][:, t * P : (t + 1) * P].bitcast(FP8X4),
                     lhsT_scale=w_scales[o][:, t * P : (t + 1) * P],
                     rhs=moving.bitcast(FP8X4),
-                    rhs_scale=scales[c * CHUNK // HALF][4 * o : P, cols],
+                    rhs_scale=scales[h][4 * o : P, cols],
                     start=(o == 0),
                     stop=(o == PASSES - 1),
                 )
 
-        nc.vector.tensor_copy(words[0][:], picked(word_table[0], 0, S))
-        quantize(0)
         for h in range(2):
             nc.vector.tensor_copy(scales[h][:], picked(scale_table, h * HALF, HALF))
+        quantize(0)
+        for h in range(2):
+            nc.vector.tensor_copy(words0[h][:], picked(word_table[0], h * HALF, HALF))
             for c in range(h * CHUNKS // 2, (h + 1) * CHUNKS // 2):
                 multiply(0, c)
         quantize(1)
-        words.append(keep.tile([P, S], U32, name="words1", tag="shared", align_bytes=64))
         for c in range(CHUNKS):
-            nc.vector.tensor_copy(words[1][:, c * CHUNK : (c + 1) * CHUNK], picked(word_table[1], c * CHUNK, CHUNK))
+            nc.vector.tensor_copy(words1[c][:], picked(word_table[1], c * CHUNK, CHUNK))
             multiply(1, c)
 
         result = keep.tile([P, TERM_TILES, S // D], F32, name="result")
         docs = CHUNK // D
+        active = [keep.tile([P, TERM_TILES, CHUNK], F32, name=f"active{c}") for c in range(CHUNKS)]
+        logged = [keep.tile([P, TERM_TILES, CHUNK], F32, name=f"logged{c}") for c in range(CHUNKS)]
+
+        def rectify(c, t):
+            if c * TERM_TILES + t >= CHUNKS * TERM_TILES - VECTOR_RELU:
+                nc.vector.tensor_scalar(active[c][:, t, :], acc[c][t][:], bias_cols[:, t : t + 1], 0.0, ALU.add, ALU.max)
+            else:
+                nc.scalar.activation(active[c][:, t, :], acc[c][t][:], ACT.Relu, bias=bias_cols[:, t : t + 1])
+
+        def log_and_sum(c, ts):
+            nc.scalar.activation(logged[c][:, ts, :], active[c][:, ts, :], ACT.Ln, bias=1.0)
+            sums = result[:, ts, c * docs : (c + 1) * docs]
+            values = logged[c][:, ts, :].rearrange("p t (v d) -> p t v d", d=D)
+            if c < GPSIMD_SUMS:
+                width = D
+                while width > 2:
+                    width //= 2
+                    halved = keep.tile([P, TERM_TILES, docs, width], F32, name=f"halved{c}_{width}")
+                    nc.gpsimd.tensor_tensor(halved[:], values[:, :, :, 0:width], values[:, :, :, width : 2 * width], ALU.add)
+                    values = halved[:]
+                nc.gpsimd.tensor_tensor(sums, values[:, :, :, 0], values[:, :, :, 1], ALU.add)
+            else:
+                nc.vector.tensor_reduce(sums, values, mybir.AxisListType.X, ALU.add)
+
         for c in range(CHUNKS):
-            active = keep.tile([P, TERM_TILES, CHUNK], F32, name=f"active{c}")
-            logged = keep.tile([P, TERM_TILES, CHUNK], F32, name=f"logged{c}")
             for t in range(TERM_TILES):
-                if c * TERM_TILES + t >= CHUNKS * TERM_TILES - VECTOR_RELU:
-                    nc.vector.tensor_scalar(active[:, t, :], acc[c][t][:], bias_cols[:, t : t + 1], 0.0, ALU.add, ALU.max)
-                else:
-                    nc.scalar.activation(active[:, t, :], acc[c][t][:], ACT.Relu, bias=bias_cols[:, t : t + 1])
-            nc.scalar.activation(logged[:], active[:], ACT.Ln, bias=1.0)
-            nc.vector.tensor_reduce(
-                result[:, :, c * docs : (c + 1) * docs],
-                logged[:].rearrange("p t (v d) -> p t v d", d=D),
-                mybir.AxisListType.X,
-                ALU.add,
-            )
+                rectify(c, t)
+            if c < CHUNKS - 1:
+                log_and_sum(c, slice(0, TERM_TILES))
+            else:
+                for t in range(TERM_TILES):
+                    log_and_sum(c, slice(t, t + 1))
         nc.sync.dma_start(out=out.rearrange("(t p) v -> p t v", p=P), in_=result[:])

@@ -23,8 +23,8 @@ CHUNK = 256
 CHUNKS = S // CHUNK
 HALF = S // 2
 LANES = 16
-VECTOR_RELU = 3
-GPSIMD_SUMS = 0
+VECTOR_RELU = 2
+GPSIMD_SUMS = 1
 
 
 def tile_picked_ysplade_sum_p_kernel(tc, x_words, x_scales, w1, bias, offs, out):
@@ -35,7 +35,7 @@ def tile_picked_ysplade_sum_p_kernel(tc, x_words, x_scales, w1, bias, offs, out)
 
         offsets = keep.tile([P, S // LANES], U16, name="offsets")
         word_table = [keep.tile([P, T], U32, name=f"word_table{o}", align_bytes=64) for o in range(PASSES)]
-        scale_table = keep.tile([P, T], U8, name="scale_table", align_bytes=64)
+        scale_table = keep.tile([P, T], U8, name="scale_table", tag="shared", align_bytes=64)
         w_raw = [keep.tile([P, PACK, N], F32, name=f"w_raw{o}", align_bytes=64) for o in range(PASSES)]
         bias_cols = keep.tile([P, TERM_TILES], F32, name="bias_cols")
         warm_in = keep.tile([P, 1], F32, name="warm_in")
@@ -48,25 +48,26 @@ def tile_picked_ysplade_sum_p_kernel(tc, x_words, x_scales, w1, bias, offs, out)
             nc.sync.dma_start(out=w_raw[o][:], in_=w1[512 * o : 512 * (o + 1), :].rearrange("(p j) m -> p j m", j=PACK))
 
         nc.vector.memset(scale_table[:].bitcast(I32), 0)
-        for q in range(4):
-            nc.scalar.dma_start(out=scale_table[32 * q : 32 * q + 4 * PASSES, :].bitcast(I32), in_=x_scales[:, 4 * q : 4 * q + 4, :].bitcast(I32))
-        nc.vector.memset(warm_in[:], 1.0)
+        nc.gpsimd.memset(warm_in[:], 1.0)
         nc.scalar.activation(warm_out[:], warm_in[:], ACT.Ln, bias=1.0)
-        load_weights(0)
         nc.sync.dma_start(offsets[:], offs)
+        load_weights(0)
+        for q in range(4):
+            nc.sync.dma_start(out=scale_table[32 * q : 32 * q + 4 * PASSES, :].bitcast(I32), in_=x_scales[:, 4 * q : 4 * q + 4, :].bitcast(I32))
         load_words(0)
         load_weights(1)
         load_words(1)
         with nc.allow_non_contiguous_dma(reason="one bias value a partition"):
             nc.sync.dma_start(out=bias_cols[:], in_=bias.rearrange("(t p) o -> p (t o)", p=P))
 
-        w_codes = [keep.tile([P, N], U32, name=f"w_codes{o}", align_bytes=64) for o in range(PASSES)]
+        w_codes = []
         w_scales = [keep.tile([P, N], U8, name=f"w_scales{o}", align_bytes=64) for o in range(PASSES)]
         w_grouped = [keep.tile([P, N, PACK], BF16, name=f"w_grouped{o}", align_bytes=64) for o in range(PASSES)]
         for o in range(PASSES):
             nc.scalar.copy(out=w_grouped[o][:], in_=w_raw[o][:].rearrange("p j m -> p m j"))
 
         def quantize(o):
+            w_codes.append(keep.tile([P, N], U32, name=f"w_codes{o}", tag="shared" if o == 0 else "codes", align_bytes=64))
             nc.vector.quantize_mx(out=w_codes[o][:].bitcast(FP8X4), scales=w_scales[o][:], in_=w_grouped[o][:].rearrange("p m j -> p (m j)"))
 
         def picked(table, start, count):
@@ -74,7 +75,7 @@ def tile_picked_ysplade_sum_p_kernel(tc, x_words, x_scales, w1, bias, offs, out)
 
         words0 = [keep.tile([P, HALF], U32, name=f"words0_{h}", align_bytes=64) for h in range(2)]
         words1 = [keep.tile([P, CHUNK], U32, name=f"words1_{c}", align_bytes=64) for c in range(CHUNKS)]
-        scales = [keep.tile([P, HALF], U8, name=f"scales{h}", align_bytes=64) for h in range(2)]
+        scales = keep.tile([P, S], U8, name="scales", align_bytes=64)
         acc = [[psum.tile([P, CHUNK], F32, name=f"acc{c}_{t}") for t in range(TERM_TILES)] for c in range(CHUNKS)]
 
         def multiply(o, c):
@@ -87,13 +88,12 @@ def tile_picked_ysplade_sum_p_kernel(tc, x_words, x_scales, w1, bias, offs, out)
                     lhsT=w_codes[o][:, t * P : (t + 1) * P].bitcast(FP8X4),
                     lhsT_scale=w_scales[o][:, t * P : (t + 1) * P],
                     rhs=moving.bitcast(FP8X4),
-                    rhs_scale=scales[h][4 * o : P, cols],
+                    rhs_scale=scales[4 * o : P, c * CHUNK : (c + 1) * CHUNK],
                     start=(o == 0),
                     stop=(o == PASSES - 1),
                 )
 
-        for h in range(2):
-            nc.vector.tensor_copy(scales[h][:], picked(scale_table, h * HALF, HALF))
+        nc.vector.tensor_copy(scales[:], picked(scale_table, 0, S))
         quantize(0)
         for h in range(2):
             nc.vector.tensor_copy(words0[h][:], picked(word_table[0], h * HALF, HALF))

@@ -23,7 +23,7 @@ CHUNK = 256
 CHUNKS = S // CHUNK
 HALF = S // 2
 LANES = 16
-VECTOR_RELU = 2
+VECTOR_RELU = 3
 GPSIMD_SUMS = 1
 
 
@@ -35,7 +35,7 @@ def tile_picked_ysplade_sum_p_kernel(tc, x_words, x_scales, w1, bias, offs, out)
 
         offsets = keep.tile([P, S // LANES], U16, name="offsets")
         word_table = [keep.tile([P, T], U32, name=f"word_table{o}", align_bytes=64) for o in range(PASSES)]
-        scale_table = keep.tile([P, T], U8, name="scale_table", tag="shared", align_bytes=64)
+        scale_table = keep.tile([P, T], U8, name="scale_table", align_bytes=64)
         w_raw = [keep.tile([P, PACK, N], F32, name=f"w_raw{o}", align_bytes=64) for o in range(PASSES)]
         bias_cols = keep.tile([P, TERM_TILES], F32, name="bias_cols")
         warm_in = keep.tile([P, 1], F32, name="warm_in")
@@ -51,9 +51,11 @@ def tile_picked_ysplade_sum_p_kernel(tc, x_words, x_scales, w1, bias, offs, out)
         nc.gpsimd.memset(warm_in[:], 1.0)
         nc.scalar.activation(warm_out[:], warm_in[:], ACT.Ln, bias=1.0)
         nc.sync.dma_start(offsets[:], offs)
-        load_weights(0)
+        w_rows = w1[0:512, :].rearrange("(p j) m -> p j m", j=PACK)
+        nc.sync.dma_start(out=w_raw[0][:, 0:2, :], in_=w_rows[:, 0:2, :])
         for q in range(4):
             nc.sync.dma_start(out=scale_table[32 * q : 32 * q + 4 * PASSES, :].bitcast(I32), in_=x_scales[:, 4 * q : 4 * q + 4, :].bitcast(I32))
+        nc.sync.dma_start(out=w_raw[0][:, 2:PACK, :], in_=w_rows[:, 2:PACK, :])
         load_words(0)
         load_weights(1)
         load_words(1)
@@ -67,7 +69,7 @@ def tile_picked_ysplade_sum_p_kernel(tc, x_words, x_scales, w1, bias, offs, out)
             nc.scalar.copy(out=w_grouped[o][:], in_=w_raw[o][:].rearrange("p j m -> p m j"))
 
         def quantize(o):
-            w_codes.append(keep.tile([P, N], U32, name=f"w_codes{o}", tag="shared" if o == 0 else "codes", align_bytes=64))
+            w_codes.append(keep.tile([P, N], U32, name=f"w_codes{o}", align_bytes=64))
             nc.vector.quantize_mx(out=w_codes[o][:].bitcast(FP8X4), scales=w_scales[o][:], in_=w_grouped[o][:].rearrange("p m j -> p (m j)"))
 
         def picked(table, start, count):
@@ -113,29 +115,34 @@ def tile_picked_ysplade_sum_p_kernel(tc, x_words, x_scales, w1, bias, offs, out)
             if c * TERM_TILES + t >= CHUNKS * TERM_TILES - VECTOR_RELU:
                 nc.vector.tensor_scalar(active[c][:, t, :], acc[c][t][:], bias_cols[:, t : t + 1], 0.0, ALU.add, ALU.max)
             else:
-                nc.scalar.activation(active[c][:, t, :], acc[c][t][:], ACT.Relu, bias=bias_cols[:, t : t + 1])
+                sums_in, values_out = acc[c][t][:], active[c][:, t, :]
+                if c < GPSIMD_SUMS:
+                    sums_in = sums_in.rearrange("p (v d) -> p d v", d=D)
+                    values_out = values_out.rearrange("p (d v) -> p d v", d=D)
+                nc.scalar.activation(values_out, sums_in, ACT.Relu, bias=bias_cols[:, t : t + 1])
 
         def log_and_sum(c, ts):
             nc.scalar.activation(logged[c][:, ts, :], active[c][:, ts, :], ACT.Ln, bias=1.0)
             sums = result[:, ts, c * docs : (c + 1) * docs]
             values = logged[c][:, ts, :].rearrange("p t (v d) -> p t v d", d=D)
             if c < GPSIMD_SUMS:
-                width = D
-                while width > 2:
+                values = logged[c][:]
+                width = CHUNK
+                while width > docs:
                     width //= 2
-                    halved = keep.tile([P, TERM_TILES, docs, width], F32, name=f"halved{c}_{width}")
-                    nc.gpsimd.tensor_tensor(halved[:], values[:, :, :, 0:width], values[:, :, :, width : 2 * width], ALU.add)
-                    values = halved[:]
-                nc.gpsimd.tensor_tensor(sums, values[:, :, :, 0], values[:, :, :, 1], ALU.add)
+                    halved = sums if width == docs else keep.tile([P, TERM_TILES, width], F32, name=f"halved{c}_{width}")[:]
+                    nc.gpsimd.tensor_tensor(halved, values[:, :, 0:width], values[:, :, width : 2 * width], ALU.add)
+                    values = halved
             else:
                 nc.vector.tensor_reduce(sums, values, mybir.AxisListType.X, ALU.add)
 
         for c in range(CHUNKS):
             for t in range(TERM_TILES):
                 rectify(c, t)
-            if c < CHUNKS - 1:
+            if c < 2:
                 log_and_sum(c, slice(0, TERM_TILES))
             else:
                 for t in range(TERM_TILES):
                     log_and_sum(c, slice(t, t + 1))
-        nc.sync.dma_start(out=out.rearrange("(t p) v -> p t v", p=P), in_=result[:])
+        for t in range(TERM_TILES):
+            nc.sync.dma_start(out=out[t * P : (t + 1) * P, :], in_=result[:, t, :])

from contextlib import ExitStack

import concourse.mybir as mybir

K, T, S, N, D = 1024, 2048, 1024, 256, 8
FLOPS = 2 * K * N * S

F32 = mybir.dt.float32
BF16 = mybir.dt.bfloat16
I32 = mybir.dt.int32
U32 = mybir.dt.uint32
U16 = mybir.dt.uint16
U8 = mybir.dt.uint8
FP8X4 = mybir.dt.float8_e4m3fn_x4
ACT = mybir.ActivationFunctionType
ALU = mybir.AluOpType

P = 128
PACK = 4
PASSES = K // (P * PACK)
TERM_TILES = N // P
CHUNK = 256
CHUNKS = S // CHUNK
HALF = S // 2
LANES = 16
VECTOR_RELU = 3
GPSIMD_SUMS = 1


def tile_picked_ysplade_sum_p_kernel(tc, x_words, x_scales, w1, bias, offs, out):
    nc = tc.nc
    with ExitStack() as ctx:
        keep = ctx.enter_context(tc.tile_pool(name="keep", bufs=1))
        psum = ctx.enter_context(tc.psum_pool(name="psum", bufs=1))

        offsets = keep.tile([P, S // LANES], U16, name="offsets")
        word_table = [keep.tile([P, T], U32, name=f"word_table{o}", align_bytes=64) for o in range(PASSES)]
        scale_table = keep.tile([P, T], U8, name="scale_table", align_bytes=64)
        w_raw = [keep.tile([P, PACK, N], F32, name=f"w_raw{o}", align_bytes=64) for o in range(PASSES)]
        bias_cols = keep.tile([P, TERM_TILES], F32, name="bias_cols")
        warm_in = keep.tile([P, 1], F32, name="warm_in")
        warm_out = keep.tile([P, 1], F32, name="warm_out")

        def load_words(o):
            nc.sync.dma_start(out=word_table[o][:].bitcast(I32), in_=x_words[o].rearrange("p n t -> p (n t)").bitcast(I32))

        def load_weights(o):
            nc.sync.dma_start(out=w_raw[o][:], in_=w1[512 * o : 512 * (o + 1), :].rearrange("(p j) m -> p j m", j=PACK))

        nc.vector.memset(scale_table[:].bitcast(I32), 0)
        nc.gpsimd.memset(warm_in[:], 1.0)
        nc.scalar.activation(warm_out[:], warm_in[:], ACT.Ln, bias=1.0)
        nc.sync.dma_start(offsets[:], offs)
        w_rows = w1[0:512, :].rearrange("(p j) m -> p j m", j=PACK)
        nc.sync.dma_start(out=w_raw[0][:, 0:2, :], in_=w_rows[:, 0:2, :])
        for q in range(4):
            nc.sync.dma_start(out=scale_table[32 * q : 32 * q + 4 * PASSES, :].bitcast(I32), in_=x_scales[:, 4 * q : 4 * q + 4, :].bitcast(I32))
        nc.sync.dma_start(out=w_raw[0][:, 2:PACK, :], in_=w_rows[:, 2:PACK, :])
        load_words(0)
        load_weights(1)
        load_words(1)
        with nc.allow_non_contiguous_dma(reason="one bias value a partition"):
            nc.sync.dma_start(out=bias_cols[:], in_=bias.rearrange("(t p) o -> p (t o)", p=P))

        w_codes = []
        w_scales = [keep.tile([P, N], U8, name=f"w_scales{o}", align_bytes=64) for o in range(PASSES)]
        w_grouped = [keep.tile([P, N, PACK], BF16, name=f"w_grouped{o}", align_bytes=64) for o in range(PASSES)]
        for o in range(PASSES):
            nc.scalar.copy(out=w_grouped[o][:], in_=w_raw[o][:].rearrange("p j m -> p m j"))

        def quantize(o):
            w_codes.append(keep.tile([P, N], U32, name=f"w_codes{o}", align_bytes=64))
            nc.vector.quantize_mx(out=w_codes[o][:].bitcast(FP8X4), scales=w_scales[o][:], in_=w_grouped[o][:].rearrange("p m j -> p (m j)"))

        def picked(table, start, count):
            return table[:].indirect(offsets[:, start // LANES : (start + count) // LANES])

        words0 = [keep.tile([P, HALF], U32, name=f"words0_{h}", align_bytes=64) for h in range(2)]
        words1 = [keep.tile([P, CHUNK], U32, name=f"words1_{c}", align_bytes=64) for c in range(CHUNKS)]
        scales = keep.tile([P, S], U8, name="scales", align_bytes=64)
        acc = [[psum.tile([P, CHUNK], F32, name=f"acc{c}_{t}") for t in range(TERM_TILES)] for c in range(CHUNKS)]

        def multiply(o, c):
            h = c * CHUNK // HALF
            cols = slice((c * CHUNK) % HALF, (c * CHUNK) % HALF + CHUNK)
            moving = words0[h][:, cols] if o == 0 else words1[c][:]
            for t in range(TERM_TILES):
                nc.tensor.matmul_mx(
                    out=acc[c][t][:],
                    lhsT=w_codes[o][:, t * P : (t + 1) * P].bitcast(FP8X4),
                    lhsT_scale=w_scales[o][:, t * P : (t + 1) * P],
                    rhs=moving.bitcast(FP8X4),
                    rhs_scale=scales[4 * o : P, c * CHUNK : (c + 1) * CHUNK],
                    start=(o == 0),
                    stop=(o == PASSES - 1),
                )

        nc.vector.tensor_copy(scales[:], picked(scale_table, 0, S))
        quantize(0)
        for h in range(2):
            nc.vector.tensor_copy(words0[h][:], picked(word_table[0], h * HALF, HALF))
            for c in range(h * CHUNKS // 2, (h + 1) * CHUNKS // 2):
                multiply(0, c)
        quantize(1)
        for c in range(CHUNKS):
            nc.vector.tensor_copy(words1[c][:], picked(word_table[1], c * CHUNK, CHUNK))
            multiply(1, c)

        result = keep.tile([P, TERM_TILES, S // D], F32, name="result")
        docs = CHUNK // D
        active = [keep.tile([P, TERM_TILES, CHUNK], F32, name=f"active{c}") for c in range(CHUNKS)]
        logged = [keep.tile([P, TERM_TILES, CHUNK], F32, name=f"logged{c}") for c in range(CHUNKS)]

        def rectify(c, t):
            if c * TERM_TILES + t >= CHUNKS * TERM_TILES - VECTOR_RELU:
                nc.vector.tensor_scalar(active[c][:, t, :], acc[c][t][:], bias_cols[:, t : t + 1], 0.0, ALU.add, ALU.max)
            else:
                sums_in, values_out = acc[c][t][:], active[c][:, t, :]
                if c < GPSIMD_SUMS:
                    sums_in = sums_in.rearrange("p (v d) -> p d v", d=D)
                    values_out = values_out.rearrange("p (d v) -> p d v", d=D)
                nc.scalar.activation(values_out, sums_in, ACT.Relu, bias=bias_cols[:, t : t + 1])

        def log_and_sum(c, ts):
            nc.scalar.activation(logged[c][:, ts, :], active[c][:, ts, :], ACT.Ln, bias=1.0)
            sums = result[:, ts, c * docs : (c + 1) * docs]
            values = logged[c][:, ts, :].rearrange("p t (v d) -> p t v d", d=D)
            if c < GPSIMD_SUMS:
                values = logged[c][:]
                width = CHUNK
                while width > docs:
                    width //= 2
                    halved = sums if width == docs else keep.tile([P, TERM_TILES, width], F32, name=f"halved{c}_{width}")[:]
                    nc.gpsimd.tensor_tensor(halved, values[:, :, 0:width], values[:, :, width : 2 * width], ALU.add)
                    values = halved
            else:
                nc.vector.tensor_reduce(sums, values, mybir.AxisListType.X, ALU.add)

        for c in range(CHUNKS):
            for t in range(TERM_TILES):
                rectify(c, t)
            if c < 2:
                log_and_sum(c, slice(0, TERM_TILES))
            else:
                for t in range(TERM_TILES):
                    log_and_sum(c, slice(t, t + 1))
        for t in range(TERM_TILES):
            nc.sync.dma_start(out=out[t * P : (t + 1) * P, :], in_=result[:, t, :])
